import numpy as np
import ml_dtypes


def mxq(x, axis, fmt="e4m3"):
    dtype, down = {"e4m3": (ml_dtypes.float8_e4m3fn, 7), "e5m2": (ml_dtypes.float8_e5m2, 14)}[fmt]
    v = np.moveaxis(np.asarray(x, np.float32).astype(ml_dtypes.bfloat16).astype(np.float64), axis, -1)
    blocks = v.reshape(v.shape[:-1] + (-1, 32))
    amax = np.abs(blocks).max(-1, keepdims=True)
    byte = np.maximum(np.where(amax > 0, np.frexp(amax)[1] - 1 + 127, 0) - down, 1)
    scale = np.exp2(byte - 127.0)
    codes = (blocks / scale).astype(np.float32).astype(dtype).astype(np.float64)
    return np.moveaxis((codes * scale).reshape(v.shape), -1, axis)


WIDE = False


def mx_kscale(k):
    if not WIDE:
        return np.ones(k)
    levels = np.array([10, -10, 5, -5, 0])
    if k % 512:
        return np.exp2(np.random.permutation(np.resize(levels, k // 32))).repeat(32)
    a = np.empty((k // 512, 16))
    for p in range(k // 512):
        a[p, :8] = np.random.permutation(np.resize(levels, 8))
        for g in range(8):
            far = levels[np.abs(levels - a[p, g]) >= 10]
            a[p, g + 8] = far[np.random.randint(len(far))]
    return np.exp2(a.ravel()).repeat(32)


def f64(x):
    return np.asarray(x).astype(np.float64)


def striped(idx):
    return np.tile(np.asarray(idx).reshape(-1, 16).T, (8, 1)).astype(np.uint16)


def unstriped(offs):
    return offs[:16].T.reshape(-1).astype(np.int64)


E2M1 = np.array([0.0, 0.5, 1.0, 1.5, 2.0, 3.0, 4.0, 6.0, -0.0, -0.5, -1.0, -1.5, -2.0, -3.0, -4.0, -6.0])


def pack_weight(w, fmt):
    k, n = w.shape
    w = f64(np.asarray(w, np.float32).astype(ml_dtypes.bfloat16)).reshape(k // 32, 32, n)
    amax = np.abs(w).max(1)
    if fmt == "e4m3":
        byte = np.frexp(amax)[1] - 1 + 127 - 7
    else:
        mant, ex = np.frexp(amax / 6.0)
        byte = np.where(mant > 0.5, ex, ex - 1) + 127
    byte = np.clip(np.where(amax > 0, byte, 1), 1, 254)
    scaled = (w * np.exp2(127.0 - byte)[:, None, :]).reshape(k, n).astype(np.float32)
    by_word = np.ascontiguousarray(scaled.reshape(k // 512, 128, 4, n).transpose(0, 1, 3, 2))
    if fmt == "e4m3":
        words = by_word.astype(ml_dtypes.float8_e4m3fn).view(np.uint8)
    else:
        c = by_word.astype(ml_dtypes.float4_e2m1fn).view(np.uint8) & 0xF
        words = (c[..., 0::2] | (c[..., 1::2] << 4)).reshape(k // 512, 128, 2 * n)
    return np.ascontiguousarray(words), np.ascontiguousarray(byte.astype(np.uint8).reshape(k // 512, 16, n))


def unpack_weight(words, scales, fmt):
    g, _, n = scales.shape
    words = np.ascontiguousarray(words).reshape(g, 128, n, -1)
    if fmt == "e4m3":
        vals = words.view(ml_dtypes.float8_e4m3fn).astype(np.float64)
    else:
        nib = np.empty((g, 128, n, 4), np.uint8)
        nib[..., 0::2] = words & 0xF
        nib[..., 1::2] = words >> 4
        vals = E2M1[nib]
    vals = vals * np.repeat(np.exp2(scales.astype(np.float64) - 127.0), 8, axis=1)[..., None]
    return vals.transpose(0, 1, 3, 2).reshape(g * 512, n)


D, T, I, Q, E = 512, 2048, 512, 128, 512


def setup_inputs():
    n = np.random.standard_normal
    idx = np.random.permutation(T)[:I]
    fd = mx_kscale(D)
    fi = mx_kscale(I)
    ti = np.ones(T)
    ti[idx] = fi
    keysp = pack_weight(n((D, T)) / fd[:, None], "e4m3")
    return {
        "dquery": (n((D, Q)) * 0.25 / np.sqrt(D) * fd[:, None]).astype(np.float32),
        "keys_words": keysp[0],
        "keys_scales": keysp[1],
        "olds": (0.3 * n((Q, T))).astype(np.float32),
        "keepf": (np.random.uniform(0.5, 1.0, (Q, 1))).astype(np.float32),
        "size": (np.random.uniform(0.5, 2.0, (1, I)) * fi).astype(np.float32),
        "vals": (n((E, T)) / ti).astype(np.float32),
        "offs": striped(idx),
    }


def reference(dquery, keys_words, keys_scales, olds, keepf, size, vals, offs):
    idx = unstriped(offs)
    keysu = unpack_weight(keys_words, keys_scales, "e4m3")
    dqueryq = mxq(f64(dquery), 0, "e4m3")
    keysidxg = keysu[:, idx]
    a = dqueryq.T @ keysidxg
    s = a + f64(olds)[:, idx] * f64(keepf)
    p = np.exp(s - np.max(s, axis=1, keepdims=True))
    w = p * f64(size) / np.sum(p, axis=1, keepdims=True)
    wt = w.T
    vt = f64(vals)[:, idx].T
    wtq = mxq(wt, 0, "e4m3")
    vtq = mxq(vt, 0, "e4m3")
    o = wtq.T @ vtq
    return o

@@ -1,0 +1,136 @@
+from contextlib import ExitStack
+
+import concourse.mybir as mybir
+from concourse.masks import make_identity
+
+D, T, I, Q, E = 512, 2048, 512, 128, 512
+FLOPS = 2 * Q * I * D + 2 * Q * E * I
+
+F32 = mybir.dt.float32
+BF16 = mybir.dt.bfloat16
+I32 = mybir.dt.int32
+U32 = mybir.dt.uint32
+U16 = mybir.dt.uint16
+U8 = mybir.dt.uint8
+FP8X4 = mybir.dt.float8_e4m3fn_x4
+ALU = mybir.AluOpType
+ACT = mybir.ActivationFunctionType
+
+P = 128
+PACK = 4
+
+
+def tile_attend_scorestep_kernel(tc, dquery, keys_words, keys_scales, olds, keepf, size, vals, offs, out):
+    nc = tc.nc
+    blocks = E // P
+    with ExitStack() as ctx:
+        sb = ctx.enter_context(tc.tile_pool(name="sb", bufs=1))
+        ps = ctx.enter_context(tc.psum_pool(name="ps", bufs=1))
+
+        offsets = sb.tile([P, I // 16], U16, name="offsets")
+        key_words = sb.tile([P, T], I32, name="key_words", align_bytes=64)
+        key_bytes = sb.tile([P, T], U8, name="key_bytes", align_bytes=64)
+        scale_rows = sb.tile([P, T // 4], I32, name="scale_rows", align_bytes=64)
+        dq_raw = sb.tile([P, PACK, Q], F32, name="dq_raw")
+        old_pool = sb.tile([P, T], F32, name="old_pool", align_bytes=64)
+        keep_col = sb.tile([P, 1], F32, name="keep_col")
+        size_cols = sb.tile([P, PACK], F32, name="size_cols")
+        val_pool = [sb.tile([P, T], F32, name="val_pool%d" % b, tag="pool%d" % b, align_bytes=64) for b in range(blocks)]
+        ident = sb.tile([P, P], F32, name="ident")
+
+        nc.vector.memset(key_bytes[:].bitcast(I32), 0)
+        make_identity(nc, ident[:])
+
+        nc.sync.dma_start(out=dq_raw[:], in_=dquery.rearrange("(p j) q -> p j q", j=PACK))
+        nc.sync.dma_start(offsets[:], offs)
+        for r in range(4):
+            nc.sync.dma_start(out=scale_rows[r:P:32, :], in_=keys_scales[0, r:16:4, :].bitcast(I32))
+        nc.sync.dma_start(out=key_words[:], in_=keys_words[0].rearrange("p t r -> p (t r)").bitcast(I32))
+        nc.sync.dma_start(out=size_cols[:], in_=size[0].rearrange("(p t) -> p t", t=PACK))
+        nc.sync.dma_start(out=keep_col[:], in_=keepf)
+        nc.sync.dma_start(out=old_pool[:], in_=olds)
+        for b in range(blocks):
+            nc.sync.dma_start(out=val_pool[b][:], in_=vals[b * P:(b + 1) * P, :])
+
+        size_rows = ps.tile([P, PACK, P], F32, name="size_rows")
+        for t in range(PACK):
+            nc.tensor.transpose(size_rows[:, t, :], size_cols[:, t:t + 1].to_broadcast([P, P]), ident[:])
+
+        dq_bf = sb.tile([P, Q, PACK], BF16, name="dq_bf", align_bytes=64)
+        nc.scalar.copy(out=dq_bf[:], in_=dq_raw[:].rearrange("p j q -> p q j"))
+        dq_codes = sb.tile([P, Q], U32, name="dq_codes", align_bytes=64)
+        dq_scales = sb.tile([P, Q], U8, name="dq_scales", align_bytes=64)
+
+        kg_bytes = sb.tile([P, I], U8, name="kg_bytes", align_bytes=64)
+        kg_words = sb.tile([P, I], U32, name="kg_words", align_bytes=64)
+        for quad in range(0, P, 32):
+            nc.vector.tensor_copy(out=key_bytes[quad:quad + 4, :].bitcast(I32), in_=scale_rows[quad:quad + 4, :])
+        nc.vector.quantize_mx(out=dq_codes[:].bitcast(FP8X4), scales=dq_scales[:],
+                              in_=dq_bf[:].rearrange("p q j -> p (q j)"))
+        nc.vector.tensor_copy(out=kg_bytes[:], in_=key_bytes[:].indirect(offsets[:]))
+        nc.vector.tensor_copy(out=kg_words[:], in_=key_words[:].bitcast(U32).indirect(offsets[:]))
+        scores = ps.tile([P, I], F32, name="scores")
+        nc.tensor.matmul_mx(out=scores[:], lhsT=dq_codes[:].bitcast(FP8X4), lhsT_scale=dq_scales[:],
+                            rhs=kg_words[:].bitcast(FP8X4), rhs_scale=kg_bytes[:], start=True, stop=True)
+
+        old_g = sb.tile([P, I], F32, name="old_g")
+        nc.vector.tensor_copy(out=old_g[:], in_=old_pool[:].indirect(offsets[:]))
+        s = sb.tile([P, I], F32, name="s")
+        nc.vector.scalar_tensor_tensor(out=s[:], in0=old_g[:], scalar=keep_col[:], in1=scores[:],
+                                       op0=ALU.mult, op1=ALU.add)
+        neg_max = sb.tile([P, 1], F32, name="neg_max")
+        nc.vector.tensor_reduce(out=neg_max[:], in_=s[:], axis=mybir.AxisListType.X, op=ALU.max, negate=True)
+        p = sb.tile([P, I], F32, name="p")
+        row_sum = sb.tile([P, 1], F32, name="row_sum")
+        nc.scalar.activation(out=p[:], in_=s[:], func=ACT.Exp, bias=neg_max[:], scale=1.0, accum_out=row_sum[:])
+
+        def turn(src_bf, bank_name, turned):
+            words = src_bf[:].bitcast(F32)
+            bank = ps.tile([P, 2, P], F32, name=bank_name)
+            for u in range(2):
+                nc.tensor.transpose(bank[:, u, :], words[:, u:I // 2:2], ident[:])
+            nc.scalar.copy(out=turned.bitcast(F32).rearrange("p (c u) -> p c u", u=2),
+                           in_=bank[:].rearrange("p u c -> p c u"))
+
+        def quantize(turned, name, tag):
+            width = turned.shape[1] // PACK
+            codes = sb.tile([P, width], U32, name=name + "_codes", tag=tag, align_bytes=64)
+            scales = sb.tile([P, width], U8, name=name + "_scales", align_bytes=64)
+            nc.vector.quantize_mx(out=codes[:].bitcast(FP8X4), scales=scales[:], in_=turned)
+            return codes, scales
+
+        def gather_values(b, turned):
+            g = sb.tile([P, I], BF16, name="val_g%d" % b, align_bytes=64)
+            nc.vector.tensor_copy(out=g[:], in_=val_pool[b][:].indirect(offsets[:]))
+            turn(g, "turn%d" % (b % 2), turned)
+
+        def finish(b, codes, scales):
+            acc = ps.tile([P, P], F32, name="acc%d" % (b % 2))
+            nc.tensor.matmul_mx(out=acc[:], lhsT=wv_codes[:, 0:P].bitcast(FP8X4), lhsT_scale=wv_scales[:, 0:P],
+                                rhs=codes.bitcast(FP8X4), rhs_scale=scales, start=True, stop=True)
+            res = sb.tile([P, P], F32, name="res%d" % b)
+            nc.scalar.copy(out=res[:], in_=acc[:])
+            nc.sync.dma_start(out=out[:, b * P:(b + 1) * P], in_=res[:])
+
+        wv_turned = sb.tile([P, 2 * I], BF16, name="wv_turned", align_bytes=64)
+        gather_values(0, wv_turned[:, I:2 * I])
+        inv_sum = sb.tile([P, 1], F32, name="inv_sum", tag="pool0", align_bytes=64)
+        nc.vector.reciprocal(out=inv_sum[:], in_=row_sum[:])
+        w_bf = sb.tile([P, I], BF16, name="w_bf", align_bytes=64)
+        nc.vector.scalar_tensor_tensor(out=w_bf[:].rearrange("q (s t) -> q s t", t=PACK),
+                                       in0=p[:].rearrange("q (s t) -> q s t", t=PACK), scalar=inv_sum[:],
+                                       in1=size_rows[:].rearrange("q t s -> q s t"), op0=ALU.mult, op1=ALU.mult)
+        turn(w_bf, "turn_w", wv_turned[:, 0:I])
+
+        turned = {}
+        for b in range(1, blocks):
+            turned[b] = sb.tile([P, I], BF16, name="val_t%d" % b, align_bytes=64)
+            gather_values(b, turned[b][:])
+            if b == 1:
+                wv_codes, wv_scales = quantize(wv_turned[:], "wv", "pool1")
+                finish(0, wv_codes[:, P:2 * P], wv_scales[:, P:2 * P])
+            else:
+                codes, scales = quantize(turned[b - 1][:], "val%d" % (b - 1), "pool%d" % b)
+                finish(b - 1, codes[:], scales[:])
+        codes, scales = quantize(turned[blocks - 1][:], "val_last", "val_last")
+        finish(blocks - 1, codes[:], scales[:])

@@ -73,14 +73,14 @@ def tile_attend_scorestep_kernel(tc, dquery, keys_words, keys_scales, olds, keep
         nc.tensor.matmul_mx(out=scores[:], lhsT=dq_codes[:].bitcast(FP8X4), lhsT_scale=dq_scales[:],
                             rhs=kg_words[:].bitcast(FP8X4), rhs_scale=kg_bytes[:], start=True, stop=True)
 
-        old_g = sb.tile([P, I], F32, name="old_g")
+        old_g = sb.tile([P, I], F32, name="old_g", tag="old_g", align_bytes=64)
         nc.vector.tensor_copy(out=old_g[:], in_=old_pool[:].indirect(offsets[:]))
         s = sb.tile([P, I], F32, name="s")
         nc.vector.scalar_tensor_tensor(out=s[:], in0=old_g[:], scalar=keep_col[:], in1=scores[:],
                                        op0=ALU.mult, op1=ALU.add)
         neg_max = sb.tile([P, 1], F32, name="neg_max")
         nc.vector.tensor_reduce(out=neg_max[:], in_=s[:], axis=mybir.AxisListType.X, op=ALU.max, negate=True)
-        p = sb.tile([P, I], F32, name="p")
+        p = sb.tile([P, I], F32, name="p", tag="p", align_bytes=64)
         row_sum = sb.tile([P, 1], F32, name="row_sum")
         nc.scalar.activation(out=p[:], in_=s[:], func=ACT.Exp, bias=neg_max[:], scale=1.0, accum_out=row_sum[:])
 
@@ -99,38 +99,37 @@ def tile_attend_scorestep_kernel(tc, dquery, keys_words, keys_scales, olds, keep
             nc.vector.quantize_mx(out=codes[:].bitcast(FP8X4), scales=scales[:], in_=turned)
             return codes, scales
 
-        def gather_values(b, turned):
-            g = sb.tile([P, I], BF16, name="val_g%d" % b, align_bytes=64)
+        def gather_values(b, tag, turned):
+            g = sb.tile([P, I], BF16, name="val_g%d" % b, tag=tag, align_bytes=64)
             nc.vector.tensor_copy(out=g[:], in_=val_pool[b][:].indirect(offsets[:]))
             turn(g, "turn%d" % (b % 2), turned)
 
-        def finish(b, codes, scales):
-            acc = ps.tile([P, P], F32, name="acc%d" % (b % 2))
+        def finish(first, codes, scales, copy_out):
+            width = codes.shape[1]
+            acc = ps.tile([P, width], F32, name="acc%d" % first)
             nc.tensor.matmul_mx(out=acc[:], lhsT=wv_codes[:, 0:P].bitcast(FP8X4), lhsT_scale=wv_scales[:, 0:P],
                                 rhs=codes.bitcast(FP8X4), rhs_scale=scales, start=True, stop=True)
-            res = sb.tile([P, P], F32, name="res%d" % b)
-            nc.scalar.copy(out=res[:], in_=acc[:])
-            nc.sync.dma_start(out=out[:, b * P:(b + 1) * P], in_=res[:])
+            res = sb.tile([P, width], F32, name="res%d" % first)
+            copy_out(out=res[:], in_=acc[:])
+            nc.sync.dma_start(out=out[:, first * P:first * P + width], in_=res[:])
 
         wv_turned = sb.tile([P, 2 * I], BF16, name="wv_turned", align_bytes=64)
-        gather_values(0, wv_turned[:, I:2 * I])
-        inv_sum = sb.tile([P, 1], F32, name="inv_sum", tag="pool0", align_bytes=64)
+        mid_turned = sb.tile([P, 2 * I], BF16, name="mid_turned", align_bytes=64)
+        last_turned = sb.tile([P, I], BF16, name="last_turned", align_bytes=64)
+        gather_values(0, "val_g0", wv_turned[:, I:2 * I])
+        inv_sum = sb.tile([P, 1], F32, name="inv_sum")
         nc.vector.reciprocal(out=inv_sum[:], in_=row_sum[:])
         w_bf = sb.tile([P, I], BF16, name="w_bf", align_bytes=64)
         nc.vector.scalar_tensor_tensor(out=w_bf[:].rearrange("q (s t) -> q s t", t=PACK),
                                        in0=p[:].rearrange("q (s t) -> q s t", t=PACK), scalar=inv_sum[:],
                                        in1=size_rows[:].rearrange("q t s -> q s t"), op0=ALU.mult, op1=ALU.mult)
         turn(w_bf, "turn_w", wv_turned[:, 0:I])
-
-        turned = {}
-        for b in range(1, blocks):
-            turned[b] = sb.tile([P, I], BF16, name="val_t%d" % b, align_bytes=64)
-            gather_values(b, turned[b][:])
-            if b == 1:
-                wv_codes, wv_scales = quantize(wv_turned[:], "wv", "pool1")
-                finish(0, wv_codes[:, P:2 * P], wv_scales[:, P:2 * P])
-            else:
-                codes, scales = quantize(turned[b - 1][:], "val%d" % (b - 1), "pool%d" % b)
-                finish(b - 1, codes[:], scales[:])
-        codes, scales = quantize(turned[blocks - 1][:], "val_last", "val_last")
-        finish(blocks - 1, codes[:], scales[:])
+        gather_values(1, "val_g1", mid_turned[:, 0:I])
+        wv_codes, wv_scales = quantize(wv_turned[:], "wv", "wv_codes")
+        finish(0, wv_codes[:, P:2 * P], wv_scales[:, P:2 * P], nc.scalar.copy)
+        gather_values(2, "val_g2", mid_turned[:, I:2 * I])
+        gather_values(3, "val_g3", last_turned[:])
+        mid_codes, mid_scales = quantize(mid_turned[:], "mid", "pool3")
+        finish(1, mid_codes[:], mid_scales[:], nc.scalar.copy)
+        last_codes, last_scales = quantize(last_turned[:], "last", "last_codes")
+        finish(3, last_codes[:], last_scales[:], nc.vector.tensor_copy)

@@ -30,7 +30,6 @@ def tile_attend_scorestep_kernel(tc, dquery, keys_words, keys_scales, olds, keep
         offsets = sb.tile([P, I // 16], U16, name="offsets")
         key_words = sb.tile([P, T], I32, name="key_words", align_bytes=64)
         key_bytes = sb.tile([P, T], U8, name="key_bytes", align_bytes=64)
-        scale_rows = sb.tile([P, T // 4], I32, name="scale_rows", align_bytes=64)
         dq_raw = sb.tile([P, PACK, Q], F32, name="dq_raw")
         old_pool = sb.tile([P, T], F32, name="old_pool", align_bytes=64)
         keep_col = sb.tile([P, 1], F32, name="keep_col")
@@ -38,16 +37,16 @@ def tile_attend_scorestep_kernel(tc, dquery, keys_words, keys_scales, olds, keep
         val_pool = [sb.tile([P, T], F32, name="val_pool%d" % b, tag="pool%d" % b, align_bytes=64) for b in range(blocks)]
         ident = sb.tile([P, P], F32, name="ident")
 
-        nc.vector.memset(key_bytes[:].bitcast(I32), 0)
+        nc.gpsimd.memset(key_bytes[:].bitcast(I32), 0)
         make_identity(nc, ident[:])
 
         nc.sync.dma_start(out=dq_raw[:], in_=dquery.rearrange("(p j) q -> p j q", j=PACK))
         nc.sync.dma_start(offsets[:], offs)
-        for r in range(4):
-            nc.sync.dma_start(out=scale_rows[r:P:32, :], in_=keys_scales[0, r:16:4, :].bitcast(I32))
-        nc.sync.dma_start(out=key_words[:], in_=keys_words[0].rearrange("p t r -> p (t r)").bitcast(I32))
         nc.sync.dma_start(out=size_cols[:], in_=size[0].rearrange("(p t) -> p t", t=PACK))
         nc.sync.dma_start(out=keep_col[:], in_=keepf)
+        nc.sync.dma_start(out=key_words[:], in_=keys_words[0].rearrange("p t r -> p (t r)").bitcast(I32))
+        for r in range(4):
+            nc.sync.dma_start(out=key_bytes[r:P:32, :].bitcast(I32), in_=keys_scales[0, r:16:4, :].bitcast(I32))
         nc.sync.dma_start(out=old_pool[:], in_=olds)
         for b in range(blocks):
             nc.sync.dma_start(out=val_pool[b][:], in_=vals[b * P:(b + 1) * P, :])
@@ -63,12 +62,10 @@ def tile_attend_scorestep_kernel(tc, dquery, keys_words, keys_scales, olds, keep
 
         kg_bytes = sb.tile([P, I], U8, name="kg_bytes", align_bytes=64)
         kg_words = sb.tile([P, I], U32, name="kg_words", align_bytes=64)
-        for quad in range(0, P, 32):
-            nc.vector.tensor_copy(out=key_bytes[quad:quad + 4, :].bitcast(I32), in_=scale_rows[quad:quad + 4, :])
         nc.vector.quantize_mx(out=dq_codes[:].bitcast(FP8X4), scales=dq_scales[:],
                               in_=dq_bf[:].rearrange("p q j -> p (q j)"))
-        nc.vector.tensor_copy(out=kg_bytes[:], in_=key_bytes[:].indirect(offsets[:]))
         nc.vector.tensor_copy(out=kg_words[:], in_=key_words[:].bitcast(U32).indirect(offsets[:]))
+        nc.vector.tensor_copy(out=kg_bytes[:], in_=key_bytes[:].indirect(offsets[:]))
         scores = ps.tile([P, I], F32, name="scores")
         nc.tensor.matmul_mx(out=scores[:], lhsT=dq_codes[:].bitcast(FP8X4), lhsT_scale=dq_scales[:],
                             rhs=kg_words[:].bitcast(FP8X4), rhs_scale=kg_bytes[:], start=True, stop=True)
@@ -125,11 +122,25 @@ def tile_attend_scorestep_kernel(tc, dquery, keys_words, keys_scales, olds, keep
                                        in1=size_rows[:].rearrange("q t s -> q s t"), op0=ALU.mult, op1=ALU.mult)
         turn(w_bf, "turn_w", wv_turned[:, 0:I])
         gather_values(1, "val_g1", mid_turned[:, 0:I])
-        wv_codes, wv_scales = quantize(wv_turned[:], "wv", "wv_codes")
+        wv_codes, wv_scales = quantize(wv_turned[:], "wv", "pool1")
         finish(0, wv_codes[:, P:2 * P], wv_scales[:, P:2 * P], nc.scalar.copy)
         gather_values(2, "val_g2", mid_turned[:, I:2 * I])
-        gather_values(3, "val_g3", last_turned[:])
+        g = sb.tile([P, I], BF16, name="val_g3", align_bytes=64)
+        nc.vector.tensor_copy(out=g[:], in_=val_pool[3][:].indirect(offsets[:]))
+        bank = ps.tile([P, 2, P], F32, name="turn1")
+        for u in range(2):
+            nc.tensor.transpose(bank[:, u, :], g[:].bitcast(F32)[:, u:I // 2:2], ident[:])
+        half = P // 2
+        for h in range(2):
+            nc.scalar.copy(out=last_turned[:, h * half * PACK:(h + 1) * half * PACK].bitcast(F32).rearrange("p (c u) -> p c u", u=2),
+                           in_=bank[:, :, h * half:(h + 1) * half].rearrange("p u c -> p c u"))
         mid_codes, mid_scales = quantize(mid_turned[:], "mid", "pool3")
         finish(1, mid_codes[:], mid_scales[:], nc.scalar.copy)
-        last_codes, last_scales = quantize(last_turned[:], "last", "last_codes")
-        finish(3, last_codes[:], last_scales[:], nc.vector.tensor_copy)
+        res = sb.tile([P, P], F32, name="res3")
+        for h in range(2):
+            codes, scales = quantize(last_turned[:, h * half * PACK:(h + 1) * half * PACK], "last%d" % h, "last_codes%d" % h)
+            acc = ps.tile([P, half], F32, name="acc_last%d" % h, tag=("scores", "size_rows")[h])
+            nc.tensor.matmul_mx(out=acc[:], lhsT=wv_codes[:, 0:P].bitcast(FP8X4), lhsT_scale=wv_scales[:, 0:P],
+                                rhs=codes[:].bitcast(FP8X4), rhs_scale=scales[:], start=True, stop=True)
+            (nc.scalar.copy, nc.vector.tensor_copy)[h](out=res[:, h * half:(h + 1) * half], in_=acc[:])
+        nc.sync.dma_start(out=out[:, 3 * P:4 * P], in_=res[:])

from contextlib import ExitStack

import concourse.mybir as mybir
from concourse.masks import make_identity

D, T, I, Q, E = 512, 2048, 512, 128, 512
FLOPS = 2 * Q * I * D + 2 * Q * E * I

F32 = mybir.dt.float32
BF16 = mybir.dt.bfloat16
I32 = mybir.dt.int32
U32 = mybir.dt.uint32
U16 = mybir.dt.uint16
U8 = mybir.dt.uint8
FP8X4 = mybir.dt.float8_e4m3fn_x4
ALU = mybir.AluOpType
ACT = mybir.ActivationFunctionType

P = 128
PACK = 4


def tile_attend_scorestep_kernel(tc, dquery, keys_words, keys_scales, olds, keepf, size, vals, offs, out):
    nc = tc.nc
    blocks = E // P
    with ExitStack() as ctx:
        sb = ctx.enter_context(tc.tile_pool(name="sb", bufs=1))
        ps = ctx.enter_context(tc.psum_pool(name="ps", bufs=1))

        offsets = sb.tile([P, I // 16], U16, name="offsets")
        key_words = sb.tile([P, T], I32, name="key_words", align_bytes=64)
        key_bytes = sb.tile([P, T], U8, name="key_bytes", align_bytes=64)
        dq_raw = sb.tile([P, PACK, Q], F32, name="dq_raw")
        old_pool = sb.tile([P, T], F32, name="old_pool", align_bytes=64)
        keep_col = sb.tile([P, 1], F32, name="keep_col")
        size_cols = sb.tile([P, PACK], F32, name="size_cols")
        val_pool = [sb.tile([P, T], F32, name="val_pool%d" % b, tag="pool%d" % b, align_bytes=64) for b in range(blocks)]
        ident = sb.tile([P, P], F32, name="ident")

        nc.gpsimd.memset(key_bytes[:].bitcast(I32), 0)
        make_identity(nc, ident[:])

        nc.sync.dma_start(out=dq_raw[:], in_=dquery.rearrange("(p j) q -> p j q", j=PACK))
        nc.sync.dma_start(offsets[:], offs)
        nc.sync.dma_start(out=size_cols[:], in_=size[0].rearrange("(p t) -> p t", t=PACK))
        nc.sync.dma_start(out=keep_col[:], in_=keepf)
        nc.sync.dma_start(out=key_words[:], in_=keys_words[0].rearrange("p t r -> p (t r)").bitcast(I32))
        for r in range(4):
            nc.sync.dma_start(out=key_bytes[r:P:32, :].bitcast(I32), in_=keys_scales[0, r:16:4, :].bitcast(I32))
        nc.sync.dma_start(out=old_pool[:], in_=olds)
        for b in range(blocks):
            nc.sync.dma_start(out=val_pool[b][:], in_=vals[b * P:(b + 1) * P, :])

        size_rows = ps.tile([P, PACK, P], F32, name="size_rows")
        for t in range(PACK):
            nc.tensor.transpose(size_rows[:, t, :], size_cols[:, t:t + 1].to_broadcast([P, P]), ident[:])

        dq_bf = sb.tile([P, Q, PACK], BF16, name="dq_bf", align_bytes=64)
        nc.scalar.copy(out=dq_bf[:], in_=dq_raw[:].rearrange("p j q -> p q j"))
        dq_codes = sb.tile([P, Q], U32, name="dq_codes", align_bytes=64)
        dq_scales = sb.tile([P, Q], U8, name="dq_scales", align_bytes=64)

        kg_bytes = sb.tile([P, I], U8, name="kg_bytes", align_bytes=64)
        kg_words = sb.tile([P, I], U32, name="kg_words", align_bytes=64)
        nc.vector.quantize_mx(out=dq_codes[:].bitcast(FP8X4), scales=dq_scales[:],
                              in_=dq_bf[:].rearrange("p q j -> p (q j)"))
        nc.vector.tensor_copy(out=kg_words[:], in_=key_words[:].bitcast(U32).indirect(offsets[:]))
        nc.vector.tensor_copy(out=kg_bytes[:], in_=key_bytes[:].indirect(offsets[:]))
        scores = ps.tile([P, I], F32, name="scores")
        nc.tensor.matmul_mx(out=scores[:], lhsT=dq_codes[:].bitcast(FP8X4), lhsT_scale=dq_scales[:],
                            rhs=kg_words[:].bitcast(FP8X4), rhs_scale=kg_bytes[:], start=True, stop=True)

        old_g = sb.tile([P, I], F32, name="old_g", tag="old_g", align_bytes=64)
        nc.vector.tensor_copy(out=old_g[:], in_=old_pool[:].indirect(offsets[:]))
        s = sb.tile([P, I], F32, name="s")
        nc.vector.scalar_tensor_tensor(out=s[:], in0=old_g[:], scalar=keep_col[:], in1=scores[:],
                                       op0=ALU.mult, op1=ALU.add)
        neg_max = sb.tile([P, 1], F32, name="neg_max")
        nc.vector.tensor_reduce(out=neg_max[:], in_=s[:], axis=mybir.AxisListType.X, op=ALU.max, negate=True)
        p = sb.tile([P, I], F32, name="p", tag="p", align_bytes=64)
        row_sum = sb.tile([P, 1], F32, name="row_sum")
        nc.scalar.activation(out=p[:], in_=s[:], func=ACT.Exp, bias=neg_max[:], scale=1.0, accum_out=row_sum[:])

        def turn(src_bf, bank_name, turned):
            words = src_bf[:].bitcast(F32)
            bank = ps.tile([P, 2, P], F32, name=bank_name)
            for u in range(2):
                nc.tensor.transpose(bank[:, u, :], words[:, u:I // 2:2], ident[:])
            nc.scalar.copy(out=turned.bitcast(F32).rearrange("p (c u) -> p c u", u=2),
                           in_=bank[:].rearrange("p u c -> p c u"))

        def quantize(turned, name, tag):
            width = turned.shape[1] // PACK
            codes = sb.tile([P, width], U32, name=name + "_codes", tag=tag, align_bytes=64)
            scales = sb.tile([P, width], U8, name=name + "_scales", align_bytes=64)
            nc.vector.quantize_mx(out=codes[:].bitcast(FP8X4), scales=scales[:], in_=turned)
            return codes, scales

        def gather_values(b, tag, turned):
            g = sb.tile([P, I], BF16, name="val_g%d" % b, tag=tag, align_bytes=64)
            nc.vector.tensor_copy(out=g[:], in_=val_pool[b][:].indirect(offsets[:]))
            turn(g, "turn%d" % (b % 2), turned)

        def finish(first, codes, scales, copy_out):
            width = codes.shape[1]
            acc = ps.tile([P, width], F32, name="acc%d" % first)
            nc.tensor.matmul_mx(out=acc[:], lhsT=wv_codes[:, 0:P].bitcast(FP8X4), lhsT_scale=wv_scales[:, 0:P],
                                rhs=codes.bitcast(FP8X4), rhs_scale=scales, start=True, stop=True)
            res = sb.tile([P, width], F32, name="res%d" % first)
            copy_out(out=res[:], in_=acc[:])
            nc.sync.dma_start(out=out[:, first * P:first * P + width], in_=res[:])

        wv_turned = sb.tile([P, 2 * I], BF16, name="wv_turned", align_bytes=64)
        mid_turned = sb.tile([P, 2 * I], BF16, name="mid_turned", align_bytes=64)
        last_turned = sb.tile([P, I], BF16, name="last_turned", align_bytes=64)
        gather_values(0, "val_g0", wv_turned[:, I:2 * I])
        inv_sum = sb.tile([P, 1], F32, name="inv_sum")
        nc.vector.reciprocal(out=inv_sum[:], in_=row_sum[:])
        w_bf = sb.tile([P, I], BF16, name="w_bf", align_bytes=64)
        nc.vector.scalar_tensor_tensor(out=w_bf[:].rearrange("q (s t) -> q s t", t=PACK),
                                       in0=p[:].rearrange("q (s t) -> q s t", t=PACK), scalar=inv_sum[:],
                                       in1=size_rows[:].rearrange("q t s -> q s t"), op0=ALU.mult, op1=ALU.mult)
        turn(w_bf, "turn_w", wv_turned[:, 0:I])
        gather_values(1, "val_g1", mid_turned[:, 0:I])
        wv_codes, wv_scales = quantize(wv_turned[:], "wv", "pool1")
        finish(0, wv_codes[:, P:2 * P], wv_scales[:, P:2 * P], nc.scalar.copy)
        gather_values(2, "val_g2", mid_turned[:, I:2 * I])
        g = sb.tile([P, I], BF16, name="val_g3", align_bytes=64)
        nc.vector.tensor_copy(out=g[:], in_=val_pool[3][:].indirect(offsets[:]))
        bank = ps.tile([P, 2, P], F32, name="turn1")
        for u in range(2):
            nc.tensor.transpose(bank[:, u, :], g[:].bitcast(F32)[:, u:I // 2:2], ident[:])
        half = P // 2
        for h in range(2):
            nc.scalar.copy(out=last_turned[:, h * half * PACK:(h + 1) * half * PACK].bitcast(F32).rearrange("p (c u) -> p c u", u=2),
                           in_=bank[:, :, h * half:(h + 1) * half].rearrange("p u c -> p c u"))
        mid_codes, mid_scales = quantize(mid_turned[:], "mid", "pool3")
        finish(1, mid_codes[:], mid_scales[:], nc.scalar.copy)
        res = sb.tile([P, P], F32, name="res3")
        for h in range(2):
            codes, scales = quantize(last_turned[:, h * half * PACK:(h + 1) * half * PACK], "last%d" % h, "last_codes%d" % h)
            acc = ps.tile([P, half], F32, name="acc_last%d" % h, tag=("scores", "size_rows")[h])
            nc.tensor.matmul_mx(out=acc[:], lhsT=wv_codes[:, 0:P].bitcast(FP8X4), lhsT_scale=wv_scales[:, 0:P],
                                rhs=codes[:].bitcast(FP8X4), rhs_scale=scales[:], start=True, stop=True)
            (nc.scalar.copy, nc.vector.tensor_copy)[h](out=res[:, h * half:(h + 1) * half], in_=acc[:])
        nc.sync.dma_start(out=out[:, 3 * P:4 * P], in_=res[:])
